import numpy as np
import ml_dtypes

BF16 = ml_dtypes.bfloat16


def bf(x):
    return np.asarray(x, np.float32).astype(BF16)


def f32(x):
    return np.asarray(x, np.float32)


def f64(x):
    return np.asarray(x).astype(np.float64)


def striped(idx):
    return np.tile(idx.reshape(-1, 16).T, (8, 1))


S, K, M, N = 512, 512, 128, 128


def setup_inputs():
    return {"base": bf(np.random.standard_normal((M, S))), "x": bf(np.random.standard_normal((K, N))), "w": bf(np.random.standard_normal((K, M)) / np.sqrt(K)), "s": f32(0.5 + np.random.random_sample((M, 1))), "b": f32(0.5 * np.random.standard_normal((M, 1))), "offs": striped(np.random.permutation(S)[:N])}


def reference(base, x, w, s, b, offs):
    idx = offs[:16].T.reshape(-1)
    z = f64(base).copy()
    z[:, idx] += f64(w).T @ f64(x)
    return z * f64(s) + f64(b)

@@ -1,0 +1,47 @@
+import concourse.mybir as mybir
+from concourse.masks import make_identity
+
+BF16, F32, U16 = mybir.dt.bfloat16, mybir.dt.float32, mybir.dt.uint16
+MULT, ADD = mybir.AluOpType.mult, mybir.AluOpType.add
+
+P = 128
+S = 512
+K = 512
+N = 128
+BLOCKS = K // P
+
+FLOPS = 2 * K * P * N
+
+
+def tile_scatter_matmul_kernel(tc, base, x, w, s, b, offs, out):
+    nc = tc.nc
+    with (
+        tc.tile_pool(name="held", bufs=1) as held,
+        tc.psum_pool(name="psum", bufs=1) as psum,
+    ):
+        base_tile = held.tile([P, S], BF16)
+        w_tile = held.tile([P, BLOCKS, P], BF16)
+        x_tile = held.tile([P, BLOCKS, N], BF16)
+        offsets = held.tile([P, N // 16], U16)
+        gain = held.tile([P, 1], F32)
+        shift = held.tile([P, 1], F32)
+        ident = held.tile([P, P], BF16)
+        result = held.tile([P, S], F32)
+        window = psum.tile([P, S], F32)
+
+        nc.sync.dma_start(base_tile[:], base)
+        nc.sync.dma_start(offsets[:], offs)
+        nc.sync.dma_start(w_tile[:], w.rearrange("(p a) m -> p a m", a=BLOCKS))
+        nc.sync.dma_start(x_tile[:], x.rearrange("(p a) n -> p a n", a=BLOCKS))
+        nc.scalar.dma_start(gain[:], s)
+        nc.scalar.dma_start(shift[:], b)
+        make_identity(nc, ident[:])
+
+        nc.tensor.matmul(window[:], ident[:], base_tile[:], start=True, stop=False)
+        for a in range(BLOCKS):
+            nc.tensor.matmul(
+                window[:].indirect(offsets[:]), w_tile[:, a, :], x_tile[:, a, :], start=False, stop=a == BLOCKS - 1
+            )
+
+        nc.vector.tensor_scalar(result[:], window[:], gain[:], shift[:], MULT, ADD)
+        nc.sync.dma_start(out, result[:])

@@ -9,6 +9,7 @@ S = 512
 K = 512
 N = 128
 BLOCKS = K // P
+WARM_UPS = 4
 
 FLOPS = 2 * K * P * N
 
@@ -27,7 +28,9 @@ def tile_scatter_matmul_kernel(tc, base, x, w, s, b, offs, out):
         shift = held.tile([P, 1], F32)
         ident = held.tile([P, P], BF16)
         result = held.tile([P, S], F32)
+        zeros = held.tile([P, S], BF16)
         window = psum.tile([P, S], F32)
+        spare = psum.tile([P, S], F32)
 
         nc.sync.dma_start(base_tile[:], base)
         nc.sync.dma_start(offsets[:], offs)
@@ -36,6 +39,10 @@ def tile_scatter_matmul_kernel(tc, base, x, w, s, b, offs, out):
         nc.scalar.dma_start(gain[:], s)
         nc.scalar.dma_start(shift[:], b)
         make_identity(nc, ident[:])
+
+        nc.vector.memset(zeros[:], 0.0)
+        for turn in range(WARM_UPS):
+            nc.tensor.matmul(spare[:], zeros[:, :P], zeros[:], start=True, stop=True)
 
         nc.tensor.matmul(window[:], ident[:], base_tile[:], start=True, stop=False)
         for a in range(BLOCKS):

@@ -36,8 +36,8 @@ def tile_scatter_matmul_kernel(tc, base, x, w, s, b, offs, out):
         nc.sync.dma_start(offsets[:], offs)
         nc.sync.dma_start(w_tile[:], w.rearrange("(p a) m -> p a m", a=BLOCKS))
         nc.sync.dma_start(x_tile[:], x.rearrange("(p a) n -> p a n", a=BLOCKS))
-        nc.scalar.dma_start(gain[:], s)
-        nc.scalar.dma_start(shift[:], b)
+        nc.sync.dma_start(gain[:], s)
+        nc.sync.dma_start(shift[:], b)
         make_identity(nc, ident[:])
 
         nc.vector.memset(zeros[:], 0.0)

import concourse.mybir as mybir
from concourse.masks import make_identity

BF16, F32, U16 = mybir.dt.bfloat16, mybir.dt.float32, mybir.dt.uint16
MULT, ADD = mybir.AluOpType.mult, mybir.AluOpType.add

P = 128
S = 512
K = 512
N = 128
BLOCKS = K // P
WARM_UPS = 4

FLOPS = 2 * K * P * N


def tile_scatter_matmul_kernel(tc, base, x, w, s, b, offs, out):
    nc = tc.nc
    with (
        tc.tile_pool(name="held", bufs=1) as held,
        tc.psum_pool(name="psum", bufs=1) as psum,
    ):
        base_tile = held.tile([P, S], BF16)
        w_tile = held.tile([P, BLOCKS, P], BF16)
        x_tile = held.tile([P, BLOCKS, N], BF16)
        offsets = held.tile([P, N // 16], U16)
        gain = held.tile([P, 1], F32)
        shift = held.tile([P, 1], F32)
        ident = held.tile([P, P], BF16)
        result = held.tile([P, S], F32)
        zeros = held.tile([P, S], BF16)
        window = psum.tile([P, S], F32)
        spare = psum.tile([P, S], F32)

        nc.sync.dma_start(base_tile[:], base)
        nc.sync.dma_start(offsets[:], offs)
        nc.sync.dma_start(w_tile[:], w.rearrange("(p a) m -> p a m", a=BLOCKS))
        nc.sync.dma_start(x_tile[:], x.rearrange("(p a) n -> p a n", a=BLOCKS))
        nc.sync.dma_start(gain[:], s)
        nc.sync.dma_start(shift[:], b)
        make_identity(nc, ident[:])

        nc.vector.memset(zeros[:], 0.0)
        for turn in range(WARM_UPS):
            nc.tensor.matmul(spare[:], zeros[:, :P], zeros[:], start=True, stop=True)

        nc.tensor.matmul(window[:], ident[:], base_tile[:], start=True, stop=False)
        for a in range(BLOCKS):
            nc.tensor.matmul(
                window[:].indirect(offsets[:]), w_tile[:, a, :], x_tile[:, a, :], start=False, stop=a == BLOCKS - 1
            )

        nc.vector.tensor_scalar(result[:], window[:], gain[:], shift[:], MULT, ADD)
        nc.sync.dma_start(out, result[:])
